import numpy as np
CORES = [20,148,276,404,108,236,364,492]
N = 8
def setup_inputs(rng):
    return {"x": rng.standard_normal((N, 128 // N, 128), dtype=np.float32)}
def reference(x):
    g = np.concatenate(list(x), axis=0)
    return {"y": np.broadcast_to(g, (N,) + g.shape)}

@@ -1,0 +1,84 @@
+import concourse.bass as bass
+
+SCRATCH = {
+    "gather": ("dram", [8, 128, 16], "float32"),
+}
+SEMAPHORES = ["local", "arrived", "sent"]
+
+CHIPS = (2, 13)
+RANK_CORE = 4
+RELAY_A = 6
+RELAY_B = 7
+OFF = 0x00FF
+
+
+def world(h, c, k):
+    return 128 * h + 8 * c + k
+
+
+def piece_of(h, c):
+    return h + 4 * CHIPS.index(c)
+
+
+def outgoing(core):
+    h, c, k = core // 128, (core % 128) // 8, core % 8
+    if c not in CHIPS:
+        return None
+    o = 15 - c
+    a1, a2 = h ^ 1, 3 - h
+    if k == RANK_CORE:
+        return piece_of(h, c), [(OFF, [world(a2, c, RELAY_B), world(h, c, RELAY_A), world(a1, c, RANK_CORE)])]
+    if k == RELAY_A:
+        return piece_of(h, c), [(OFF, [world(h, o, RANK_CORE), world(a1, o, RANK_CORE)])]
+    if k == RELAY_B:
+        return piece_of(a2, c), [(OFF, [world(a1, c, RANK_CORE), world(h, o, RANK_CORE), world(a1, o, RANK_CORE),
+                                        world(h, c, RANK_CORE)])]
+    return None
+
+
+def engines(mask):
+    return bin(mask).count("1")
+
+
+def incoming(core):
+    total = 0
+    for h in range(4):
+        for c in CHIPS:
+            for k in (RANK_CORE, RELAY_A, RELAY_B):
+                for mask, dsts in outgoing(world(h, c, k))[1]:
+                    total += engines(mask) * dsts.count(core)
+    return total
+
+
+def send(g, core, T, topo):
+    piece, groups = outgoing(core)
+    transfers = []
+    left = 0
+    for mask, dsts in groups:
+        ids = []
+        for d in dsts:
+            rid, pid = topo.addr(d, core)
+            ids.append(bass.DstId(rid=rid, pnc=pid))
+        transfers.append(bass.RemoteDMATransfer(dst_ids=ids, dma_engine_mask=mask, remote_sem=T.sem.arrived,
+                                                srcs=[T.gather[piece]], dsts=[T.gather[piece] for d in dsts]))
+        left += engines(mask)
+    g.remote_dma_fused(transfers, local_sem=T.sem.sent)
+    return left
+
+
+def rank_program(g, core, T, topo):
+    if outgoing(core) is None:
+        return
+    rank = T.rank_of(core)
+    if rank is None:
+        g.wait_ge(T.sem.arrived, incoming(core))
+        left = send(g, core, T, topo)
+        g.wait_ge(T.sem.sent, left)
+        return
+    g.dma_start(T.gather[rank], T.x[:]).then_inc(T.sem.local, 16)
+    g.wait_ge(T.sem.local, 16)
+    left = send(g, core, T, topo)
+    g.wait_ge(T.sem.arrived, incoming(core))
+    g.dma_start(T.y[:], T.gather[:]).then_inc(T.sem.local, 16)
+    g.wait_ge(T.sem.sent, left)
+    g.wait_ge(T.sem.local, 32)

@@ -9,6 +9,7 @@ CHIPS = (2, 13)
 RANK_CORE = 4
 RELAY_A = 6
 RELAY_B = 7
+SENDERS = (RANK_CORE, RELAY_A, RELAY_B)
 OFF = 0x00FF
 
 
@@ -31,7 +32,7 @@ def outgoing(core):
     if k == RELAY_A:
         return piece_of(h, c), [(OFF, [world(h, o, RANK_CORE), world(a1, o, RANK_CORE)])]
     if k == RELAY_B:
-        return piece_of(a2, c), [(OFF, [world(a1, c, RANK_CORE), world(h, o, RANK_CORE), world(a1, o, RANK_CORE),
+        return piece_of(a2, c), [(OFF, [world(h, o, RANK_CORE), world(a1, o, RANK_CORE), world(a1, c, RANK_CORE),
                                         world(h, c, RANK_CORE)])]
     return None
 
@@ -44,7 +45,7 @@ def incoming(core):
     total = 0
     for h in range(4):
         for c in CHIPS:
-            for k in (RANK_CORE, RELAY_A, RELAY_B):
+            for k in SENDERS:
                 for mask, dsts in outgoing(world(h, c, k))[1]:
                     total += engines(mask) * dsts.count(core)
     return total

import concourse.bass as bass

SCRATCH = {
    "gather": ("dram", [8, 128, 16], "float32"),
}
SEMAPHORES = ["local", "arrived", "sent"]

CHIPS = (2, 13)
RANK_CORE = 4
RELAY_A = 6
RELAY_B = 7
SENDERS = (RANK_CORE, RELAY_A, RELAY_B)
OFF = 0x00FF


def world(h, c, k):
    return 128 * h + 8 * c + k


def piece_of(h, c):
    return h + 4 * CHIPS.index(c)


def outgoing(core):
    h, c, k = core // 128, (core % 128) // 8, core % 8
    if c not in CHIPS:
        return None
    o = 15 - c
    a1, a2 = h ^ 1, 3 - h
    if k == RANK_CORE:
        return piece_of(h, c), [(OFF, [world(a2, c, RELAY_B), world(h, c, RELAY_A), world(a1, c, RANK_CORE)])]
    if k == RELAY_A:
        return piece_of(h, c), [(OFF, [world(h, o, RANK_CORE), world(a1, o, RANK_CORE)])]
    if k == RELAY_B:
        return piece_of(a2, c), [(OFF, [world(h, o, RANK_CORE), world(a1, o, RANK_CORE), world(a1, c, RANK_CORE),
                                        world(h, c, RANK_CORE)])]
    return None


def engines(mask):
    return bin(mask).count("1")


def incoming(core):
    total = 0
    for h in range(4):
        for c in CHIPS:
            for k in SENDERS:
                for mask, dsts in outgoing(world(h, c, k))[1]:
                    total += engines(mask) * dsts.count(core)
    return total


def send(g, core, T, topo):
    piece, groups = outgoing(core)
    transfers = []
    left = 0
    for mask, dsts in groups:
        ids = []
        for d in dsts:
            rid, pid = topo.addr(d, core)
            ids.append(bass.DstId(rid=rid, pnc=pid))
        transfers.append(bass.RemoteDMATransfer(dst_ids=ids, dma_engine_mask=mask, remote_sem=T.sem.arrived,
                                                srcs=[T.gather[piece]], dsts=[T.gather[piece] for d in dsts]))
        left += engines(mask)
    g.remote_dma_fused(transfers, local_sem=T.sem.sent)
    return left


def rank_program(g, core, T, topo):
    if outgoing(core) is None:
        return
    rank = T.rank_of(core)
    if rank is None:
        g.wait_ge(T.sem.arrived, incoming(core))
        left = send(g, core, T, topo)
        g.wait_ge(T.sem.sent, left)
        return
    g.dma_start(T.gather[rank], T.x[:]).then_inc(T.sem.local, 16)
    g.wait_ge(T.sem.local, 16)
    left = send(g, core, T, topo)
    g.wait_ge(T.sem.arrived, incoming(core))
    g.dma_start(T.y[:], T.gather[:]).then_inc(T.sem.local, 16)
    g.wait_ge(T.sem.sent, left)
    g.wait_ge(T.sem.local, 32)
